import numpy as np
import ml_dtypes


def mxq(x, axis, fmt="e4m3"):
    dtype, down = {"e4m3": (ml_dtypes.float8_e4m3fn, 7), "e5m2": (ml_dtypes.float8_e5m2, 14)}[fmt]
    v = np.moveaxis(np.asarray(x, np.float32).astype(ml_dtypes.bfloat16).astype(np.float64), axis, -1)
    blocks = v.reshape(v.shape[:-1] + (-1, 32))
    amax = np.abs(blocks).max(-1, keepdims=True)
    byte = np.maximum(np.where(amax > 0, np.frexp(amax)[1] - 1 + 127, 0) - down, 1)
    scale = np.exp2(byte - 127.0)
    codes = (blocks / scale).astype(np.float32).astype(dtype).astype(np.float64)
    return np.moveaxis((codes * scale).reshape(v.shape), -1, axis)


WIDE = False


def mx_kscale(k):
    if not WIDE:
        return np.ones(k)
    levels = np.array([10, -10, 5, -5, 0])
    if k % 512:
        return np.exp2(np.random.permutation(np.resize(levels, k // 32))).repeat(32)
    a = np.empty((k // 512, 16))
    for p in range(k // 512):
        a[p, :8] = np.random.permutation(np.resize(levels, 8))
        for g in range(8):
            far = levels[np.abs(levels - a[p, g]) >= 10]
            a[p, g + 8] = far[np.random.randint(len(far))]
    return np.exp2(a.ravel()).repeat(32)


def f64(x):
    return np.asarray(x).astype(np.float64)


def striped(idx):
    return np.tile(np.asarray(idx).reshape(-1, 16).T, (8, 1)).astype(np.uint16)


def unstriped(offs):
    return offs[:16].T.reshape(-1).astype(np.int64)


E2M1 = np.array([0.0, 0.5, 1.0, 1.5, 2.0, 3.0, 4.0, 6.0, -0.0, -0.5, -1.0, -1.5, -2.0, -3.0, -4.0, -6.0])


def pack_weight(w, fmt):
    k, n = w.shape
    w = f64(np.asarray(w, np.float32).astype(ml_dtypes.bfloat16)).reshape(k // 32, 32, n)
    amax = np.abs(w).max(1)
    if fmt == "e4m3":
        byte = np.frexp(amax)[1] - 1 + 127 - 7
    else:
        mant, ex = np.frexp(amax / 6.0)
        byte = np.where(mant > 0.5, ex, ex - 1) + 127
    byte = np.clip(np.where(amax > 0, byte, 1), 1, 254)
    scaled = (w * np.exp2(127.0 - byte)[:, None, :]).reshape(k, n).astype(np.float32)
    by_word = np.ascontiguousarray(scaled.reshape(k // 512, 128, 4, n).transpose(0, 1, 3, 2))
    if fmt == "e4m3":
        words = by_word.astype(ml_dtypes.float8_e4m3fn).view(np.uint8)
    else:
        c = by_word.astype(ml_dtypes.float4_e2m1fn).view(np.uint8) & 0xF
        words = (c[..., 0::2] | (c[..., 1::2] << 4)).reshape(k // 512, 128, 2 * n)
    return np.ascontiguousarray(words), np.ascontiguousarray(byte.astype(np.uint8).reshape(k // 512, 16, n))


def unpack_weight(words, scales, fmt):
    g, _, n = scales.shape
    words = np.ascontiguousarray(words).reshape(g, 128, n, -1)
    if fmt == "e4m3":
        vals = words.view(ml_dtypes.float8_e4m3fn).astype(np.float64)
    else:
        nib = np.empty((g, 128, n, 4), np.uint8)
        nib[..., 0::2] = words & 0xF
        nib[..., 1::2] = words >> 4
        vals = E2M1[nib]
    vals = vals * np.repeat(np.exp2(scales.astype(np.float64) - 127.0), 8, axis=1)[..., None]
    return vals.transpose(0, 1, 3, 2).reshape(g * 512, n)


B, N, T, D, DV, NQ = 1, 512, 1024, 512, 128, 256
CAP = 2.0


def setup_inputs():
    n = np.random.standard_normal
    idx = np.sort(np.random.permutation(T)[:B * N].reshape(B, N), axis=1).reshape(-1)
    s = mx_kscale(D)[:, None]
    u = np.ones(T)
    u[idx] = mx_kscale(B * N)
    r = np.random.uniform(0.5, 2.0, T)
    qp = [pack_weight(x, "e4m3") for x in n((B, D, NQ)) * s * (1.00 / np.sqrt(D))]
    k = n((D, T)) / s
    v = n((DV, T)) / (u * r)
    kp = pack_weight(k, "e4m3")
    return {
        "q_words": np.stack([x[0] for x in qp]),
        "q_scales": np.stack([x[1] for x in qp]),
        "k_words": kp[0],
        "k_scales": kp[1],
        "vT": v.astype(np.float32),
        "vs": np.tile(u * r, (128, 1)).astype(np.float32),
        "offs": striped(idx),
    }


def reference(q_words, q_scales, k_words, k_scales, vT, vs, offs):
    idx = unstriped(offs)
    k = unpack_weight(k_words, k_scales, "e4m3")
    v = f64(vT)
    pick = lambda x: x[:, idx].reshape(x.shape[0], B, N).transpose(1, 0, 2)
    q = np.stack([unpack_weight(q_words[b], q_scales[b], "e4m3") for b in range(B)])
    score = q.transpose(0, 2, 1) @ pick(k)
    score = CAP * np.tanh(score / CAP)
    p = np.square(np.maximum(score, 0.0))
    total = p.sum(-1, keepdims=True) + 1.0
    w = p * pick(f64(vs))[:, :1, :]
    y = mxq(w, 2, "e4m3") @ mxq(pick(v).transpose(0, 2, 1), 1, "e4m3")
    y = y / total
    return y

@@ -1,0 +1,172 @@
+from contextlib import ExitStack
+
+import concourse.mybir as mybir
+from concourse.masks import make_identity
+
+F32 = mybir.dt.float32
+BF16 = mybir.dt.bfloat16
+I32 = mybir.dt.int32
+U32 = mybir.dt.uint32
+U16 = mybir.dt.uint16
+U8 = mybir.dt.uint8
+FP8X4 = mybir.dt.float8_e4m3fn_x4
+ACT = mybir.ActivationFunctionType
+ALU = mybir.AluOpType
+
+P = 128
+PACK = 4
+T = 1024
+N = 512
+NQ = 256
+D = 512
+DV = 128
+CAP = 2.0
+
+FLOPS = 2 * NQ * N * (D + DV)
+
+
+def tile_attend_rel2_cap_srtq256n512t1024_kernel(tc, q_words, q_scales, k_words, k_scales, vT, vs, offs, out):
+    nc = tc.nc
+    halves = NQ // P
+
+    with ExitStack() as ctx:
+        sb = ctx.enter_context(tc.tile_pool(name="sb", bufs=1))
+        ps = ctx.enter_context(tc.psum_pool(name="ps", bufs=1))
+
+        offsets = sb.tile([P, N // 16], U16, name="offsets")
+        kw_pool = sb.tile([P, T], I32, name="kw_pool", align_bytes=64)
+        ks_pool = sb.tile([P, T], U8, name="ks_pool", align_bytes=64)
+        qw = sb.tile([P, NQ], I32, name="qw", align_bytes=64)
+        qs = sb.tile([P, NQ], U8, name="qs", align_bytes=64)
+        vs_pool = sb.tile([P, T], I32, name="vs_pool", align_bytes=64)
+        warm = sb.tile([P, 8], F32, name="warm")
+        warm2 = sb.tile([P, 8], F32, name="warm2")
+
+        nc.gpsimd.memset(ks_pool[:].bitcast(I32), 0)
+        nc.gpsimd.memset(qs[:].bitcast(I32), 0)
+        nc.vector.memset(vs_pool[:], 0)
+        nc.gpsimd.memset(warm[:], 0.0)
+
+        v_raw = [sb.tile([P, T // 2], F32, name=f"v_raw{c}", align_bytes=64) for c in range(2)]
+        v_pool = sb.tile([P, T], BF16, name="v_pool", align_bytes=64)
+        for j in range(4):
+            nc.scalar.dma_start(ks_pool[j:P:32, :].bitcast(I32), k_scales[0, j:16:4, :].bitcast(I32))
+        nc.sync.dma_start(offsets[:], offs)
+        nc.sync.dma_start(kw_pool[:], k_words[0].rearrange("p n t -> p (n t)").bitcast(I32))
+        nc.sync.dma_start(qw[:], q_words[0, 0].rearrange("p n t -> p (n t)").bitcast(I32))
+        nc.sync.dma_start(v_raw[0][:], vT[:, 0 : T // 2])
+        nc.sync.dma_start(v_raw[1][:], vT[:, T // 2 : T])
+        for j in range(4):
+            nc.sync.dma_start(qs[j:P:32, :].bitcast(I32), q_scales[0, 0, j:16:4, :].bitcast(I32))
+        nc.sync.dma_start(vs_pool[0:1, :], vs[0:1, :].bitcast(I32))
+
+        nc.scalar.activation(warm2[:], warm[:], ACT.Tanh)
+
+        ident32 = sb.tile([P, P], F32, name="ident32")
+        make_identity(nc, ident32[:])
+        ident16 = sb.tile([P, P], BF16, name="ident16")
+        make_identity(nc, ident16[:])
+
+        def dealt(tile):
+            return tile[:].rearrange("p (t b i) -> p b t i", t=PACK, i=8)
+
+        ks_listed = sb.tile([P, N], U8, name="ks_listed", align_bytes=64)
+        nc.vector.tensor_copy(ks_listed[:], ks_pool[:].indirect(offsets[:]))
+        kw = sb.tile([P, N], U32, name="kw", tag="listed", align_bytes=64)
+        nc.vector.tensor_copy(dealt(kw), kw_pool[:].bitcast(U32).indirect(offsets[:]))
+        ks = sb.tile([P, N], U8, name="ks", align_bytes=64)
+        nc.vector.tensor_copy(
+            ks[:].bitcast(I32).rearrange("p (t b i) -> p t b i", t=PACK, i=2),
+            ks_listed[:].bitcast(I32).rearrange("p (b t i) -> p t b i", t=PACK, i=2),
+        )
+        vs_listed = sb.tile([P, N], U32, name="vs_listed", align_bytes=64)
+        nc.vector.tensor_copy(dealt(vs_listed), vs_pool[:].bitcast(U32).indirect(offsets[:]))
+        for c in range(2):
+            nc.scalar.activation(v_pool[:, c * T // 2 : (c + 1) * T // 2], v_raw[c][:], ACT.Copy)
+
+        score = [ps.tile([P, 2, NQ], F32, name=f"score{u}") for u in range(2)]
+        for t in range(PACK):
+            cols = slice(t * P, (t + 1) * P)
+            nc.tensor.matmul_mx(
+                out=score[t // 2][:, t % 2, :],
+                lhsT=kw[:, cols].bitcast(FP8X4),
+                lhsT_scale=ks[:, cols],
+                rhs=qw[:].bitcast(FP8X4),
+                rhs_scale=qs[:],
+                start=True,
+                stop=True,
+            )
+
+        vs_cols = ps.tile([P, PACK, P], F32, name="vs_cols")
+        for t in range(PACK):
+            nc.tensor.transpose(vs_cols[:, t, :], vs_listed[:, t * P : (t + 1) * P].bitcast(F32), ident32[:])
+
+        th = sb.tile([P, 2, NQ, 2], F32, name="th")
+        r = sb.tile([P, 2, NQ, 2], F32, name="r")
+        for u in range(2):
+            nc.scalar.activation(th[:, u], score[u][:].rearrange("p e q -> p q e"), ACT.Tanh, scale=1.0 / CAP)
+        for u in range(2):
+            flat = th[:, u].rearrange("p q e -> p (q e)")
+            nc.vector.scalar_tensor_tensor(r[:, u].rearrange("p q e -> p (q e)"), flat, 0.0, flat, ALU.max, ALU.mult)
+        v_listed = sb.tile([P, N], BF16, name="v_listed", tag="listed", align_bytes=64)
+        nc.scalar.activation(dealt(v_listed), v_pool[:].indirect(offsets[:]), ACT.Copy)
+
+        v_cols = ps.tile([P, PACK, DV], BF16, name="v_cols")
+        for t in range(PACK):
+            nc.tensor.transpose(v_cols[:, t, :], v_listed[:, t * P : (t + 1) * P], ident16[:])
+
+        sums = [ps.tile([P, P], F32, name=f"sums{h}") for h in range(halves)]
+        for u in range(2):
+            for h in range(halves):
+                for e in range(2):
+                    nc.tensor.matmul(
+                        sums[h][:],
+                        r[:, u, h * P : (h + 1) * P, e],
+                        ident32[:],
+                        start=(u == 0 and e == 0),
+                        stop=(u == 1 and e == 1),
+                        is_transpose=True,
+                    )
+
+        w = [sb.tile([P, P, 2, 2], BF16, name=f"w{h}", align_bytes=64) for h in range(halves)]
+        vs_by_slot = vs_cols[:, :, 0:1].rearrange("p (u e) x -> p x u e", u=2).to_broadcast([P, P, 2, 2])
+        for h in range(halves):
+            nc.vector.tensor_tensor(
+                w[h][:], r[:, :, h * P : (h + 1) * P, :].rearrange("p u q e -> p q u e"), vs_by_slot, ALU.mult
+            )
+
+        total = sb.tile([P, halves], F32, name="total")
+        spent = sb.tile([P, halves, P], F32, name="spent")
+        for h in range(halves):
+            nc.scalar.activation(
+                spent[:, h, :], sums[h][:], ACT.Copy, bias=1.0 / (CAP * CAP * P), accum_out=total[:, h : h + 1]
+            )
+        v_grouped = sb.tile([P, DV, PACK], BF16, name="v_grouped", align_bytes=64)
+        nc.scalar.copy(v_grouped[:], v_cols[:].rearrange("p t e -> p e t"))
+
+        w_codes = [sb.tile([P, P], U32, name=f"w_codes{h}", align_bytes=64) for h in range(halves)]
+        w_scales = [sb.tile([P, P], U8, name=f"w_scales{h}", align_bytes=64) for h in range(halves)]
+        v_codes = sb.tile([P, DV], U32, name="v_codes", align_bytes=64)
+        v_scales = sb.tile([P, DV], U8, name="v_scales", align_bytes=64)
+        inverse = sb.tile([P, halves], F32, name="inverse")
+        nc.vector.quantize_mx(w_codes[0][:].bitcast(FP8X4), w_scales[0][:], w[0][:].rearrange("p q u e -> p (q u e)"))
+        nc.vector.quantize_mx(v_codes[:].bitcast(FP8X4), v_scales[:], v_grouped[:].rearrange("p e t -> p (e t)"))
+        nc.vector.quantize_mx(w_codes[1][:].bitcast(FP8X4), w_scales[1][:], w[1][:].rearrange("p q u e -> p (q u e)"))
+        nc.vector.reciprocal(inverse[:], total[:])
+
+        y = [ps.tile([P, DV], F32, name=f"y{h}") for h in range(halves)]
+        result = [sb.tile([P, DV], F32, name=f"result{h}") for h in range(halves)]
+        for h in range(halves):
+            nc.tensor.matmul_mx(
+                out=y[h][:],
+                lhsT=w_codes[h][:].bitcast(FP8X4),
+                lhsT_scale=w_scales[h][:],
+                rhs=v_codes[:].bitcast(FP8X4),
+                rhs_scale=v_scales[:],
+                start=True,
+                stop=True,
+            )
+        nc.scalar.activation(result[0][:], y[0][:], ACT.Copy, scale=inverse[:, 0:1])
+        nc.scalar.dma_start(out[0, 0:P, :], result[0][:])
+        nc.vector.tensor_scalar(result[1][:], y[1][:], inverse[:, 1:2], None, ALU.mult)
+        nc.sync.dma_start(out[0, P:NQ, :], result[1][:])

@@ -34,11 +34,11 @@ def tile_attend_rel2_cap_srtq256n512t1024_kernel(tc, q_words, q_scales, k_words,
         ps = ctx.enter_context(tc.psum_pool(name="ps", bufs=1))
 
         offsets = sb.tile([P, N // 16], U16, name="offsets")
-        kw_pool = sb.tile([P, T], I32, name="kw_pool", align_bytes=64)
+        kw_pool = sb.tile([P, T], I32, name="kw_pool", tag="keys_then_scales", align_bytes=64)
         ks_pool = sb.tile([P, T], U8, name="ks_pool", align_bytes=64)
         qw = sb.tile([P, NQ], I32, name="qw", align_bytes=64)
         qs = sb.tile([P, NQ], U8, name="qs", align_bytes=64)
-        vs_pool = sb.tile([P, T], I32, name="vs_pool", align_bytes=64)
+        vs_pool = sb.tile([P, T], I32, name="vs_pool", tag="scales_then_values", align_bytes=64)
         warm = sb.tile([P, 8], F32, name="warm")
         warm2 = sb.tile([P, 8], F32, name="warm2")
 
@@ -47,20 +47,19 @@ def tile_attend_rel2_cap_srtq256n512t1024_kernel(tc, q_words, q_scales, k_words,
         nc.vector.memset(vs_pool[:], 0)
         nc.gpsimd.memset(warm[:], 0.0)
 
-        v_raw = [sb.tile([P, T // 2], F32, name=f"v_raw{c}", align_bytes=64) for c in range(2)]
-        v_pool = sb.tile([P, T], BF16, name="v_pool", align_bytes=64)
-        for j in range(4):
-            nc.scalar.dma_start(ks_pool[j:P:32, :].bitcast(I32), k_scales[0, j:16:4, :].bitcast(I32))
+        v_pool = sb.tile([P, T], F32, name="v_pool", align_bytes=64)
         nc.sync.dma_start(offsets[:], offs)
+        for j in range(4):
+            queue = nc.sync if j < 2 else nc.scalar
+            queue.dma_start(ks_pool[j:P:32, :].bitcast(I32), k_scales[0, j:16:4, :].bitcast(I32))
         nc.sync.dma_start(kw_pool[:], k_words[0].rearrange("p n t -> p (n t)").bitcast(I32))
         nc.sync.dma_start(qw[:], q_words[0, 0].rearrange("p n t -> p (n t)").bitcast(I32))
-        nc.sync.dma_start(v_raw[0][:], vT[:, 0 : T // 2])
-        nc.sync.dma_start(v_raw[1][:], vT[:, T // 2 : T])
-        for j in range(4):
-            nc.sync.dma_start(qs[j:P:32, :].bitcast(I32), q_scales[0, 0, j:16:4, :].bitcast(I32))
         nc.sync.dma_start(vs_pool[0:1, :], vs[0:1, :].bitcast(I32))
+        nc.sync.dma_start(v_pool[:], vT)
 
         nc.scalar.activation(warm2[:], warm[:], ACT.Tanh)
+        for j in range(4):
+            nc.scalar.dma_start(qs[j:P:32, :].bitcast(I32), q_scales[0, 0, j:16:4, :].bitcast(I32))
 
         ident32 = sb.tile([P, P], F32, name="ident32")
         make_identity(nc, ident32[:])
@@ -72,19 +71,19 @@ def tile_attend_rel2_cap_srtq256n512t1024_kernel(tc, q_words, q_scales, k_words,
 
         ks_listed = sb.tile([P, N], U8, name="ks_listed", align_bytes=64)
         nc.vector.tensor_copy(ks_listed[:], ks_pool[:].indirect(offsets[:]))
-        kw = sb.tile([P, N], U32, name="kw", tag="listed", align_bytes=64)
+        kw = sb.tile([P, N], U32, name="kw", align_bytes=64)
         nc.vector.tensor_copy(dealt(kw), kw_pool[:].bitcast(U32).indirect(offsets[:]))
         ks = sb.tile([P, N], U8, name="ks", align_bytes=64)
         nc.vector.tensor_copy(
             ks[:].bitcast(I32).rearrange("p (t b i) -> p t b i", t=PACK, i=2),
             ks_listed[:].bitcast(I32).rearrange("p (b t i) -> p t b i", t=PACK, i=2),
         )
-        vs_listed = sb.tile([P, N], U32, name="vs_listed", align_bytes=64)
+        vs_listed = sb.tile([P, N], U32, name="vs_listed", tag="keys_then_scales", align_bytes=64)
         nc.vector.tensor_copy(dealt(vs_listed), vs_pool[:].bitcast(U32).indirect(offsets[:]))
-        for c in range(2):
-            nc.scalar.activation(v_pool[:, c * T // 2 : (c + 1) * T // 2], v_raw[c][:], ACT.Copy)
+        v_listed = sb.tile([P, N], BF16, name="v_listed", tag="scales_then_values", align_bytes=64)
+        nc.vector.tensor_copy(dealt(v_listed), v_pool[:].indirect(offsets[:]))
 
-        score = [ps.tile([P, 2, NQ], F32, name=f"score{u}") for u in range(2)]
+        score = [ps.tile([P, 2, NQ], F32, name=f"score{u}", tag=f"bank{u}") for u in range(2)]
         for t in range(PACK):
             cols = slice(t * P, (t + 1) * P)
             nc.tensor.matmul_mx(
@@ -97,31 +96,36 @@ def tile_attend_rel2_cap_srtq256n512t1024_kernel(tc, q_words, q_scales, k_words,
                 stop=True,
             )
 
-        vs_cols = ps.tile([P, PACK, P], F32, name="vs_cols")
+        th_all = sb.tile([P, halves, 2, 2 * P], F32, name="th_all")
+        th = [th_all[:, h] for h in range(halves)]
+        r = [sb.tile([P, 2, 2 * P], F32, name=f"r{h}") for h in range(halves)]
+        for u in range(2):
+            nc.scalar.activation(
+                th_all[:, :, u, :].rearrange("p h (q e) -> p h q e", e=2),
+                score[u][:].rearrange("p e (h q) -> p h q e", h=halves),
+                ACT.Tanh,
+                scale=1.0 / CAP,
+            )
+        vs_cols = ps.tile([P, PACK, P], F32, name="vs_cols", tag="bank0")
         for t in range(PACK):
             nc.tensor.transpose(vs_cols[:, t, :], vs_listed[:, t * P : (t + 1) * P].bitcast(F32), ident32[:])
 
-        th = sb.tile([P, 2, NQ, 2], F32, name="th")
-        r = sb.tile([P, 2, NQ, 2], F32, name="r")
-        for u in range(2):
-            nc.scalar.activation(th[:, u], score[u][:].rearrange("p e q -> p q e"), ACT.Tanh, scale=1.0 / CAP)
-        for u in range(2):
-            flat = th[:, u].rearrange("p q e -> p (q e)")
-            nc.vector.scalar_tensor_tensor(r[:, u].rearrange("p q e -> p (q e)"), flat, 0.0, flat, ALU.max, ALU.mult)
-        v_listed = sb.tile([P, N], BF16, name="v_listed", tag="listed", align_bytes=64)
-        nc.scalar.activation(dealt(v_listed), v_pool[:].indirect(offsets[:]), ACT.Copy)
+        positive = sb.tile([P, 2, 2 * P], F32, name="positive", tag="positive_then_grouped", align_bytes=64)
+        nc.scalar.activation(positive[:], th[0][:], ACT.Relu)
+        nc.scalar.activation(r[0][:], positive[:], ACT.Square)
+        nc.vector.scalar_tensor_tensor(r[1][:], th[1][:], 0.0, th[1][:], ALU.max, ALU.mult)
 
-        v_cols = ps.tile([P, PACK, DV], BF16, name="v_cols")
+        v_cols = ps.tile([P, PACK, DV], BF16, name="v_cols", tag="bank1")
         for t in range(PACK):
             nc.tensor.transpose(v_cols[:, t, :], v_listed[:, t * P : (t + 1) * P], ident16[:])
 
         sums = [ps.tile([P, P], F32, name=f"sums{h}") for h in range(halves)]
-        for u in range(2):
-            for h in range(halves):
+        for h in (1, 0):
+            for u in range(2):
                 for e in range(2):
                     nc.tensor.matmul(
                         sums[h][:],
-                        r[:, u, h * P : (h + 1) * P, e],
+                        r[h][:, u, e : 2 * P : 2],
                         ident32[:],
                         start=(u == 0 and e == 0),
                         stop=(u == 1 and e == 1),
@@ -130,33 +134,31 @@ def tile_attend_rel2_cap_srtq256n512t1024_kernel(tc, q_words, q_scales, k_words,
 
         w = [sb.tile([P, P, 2, 2], BF16, name=f"w{h}", align_bytes=64) for h in range(halves)]
         vs_by_slot = vs_cols[:, :, 0:1].rearrange("p (u e) x -> p x u e", u=2).to_broadcast([P, P, 2, 2])
-        for h in range(halves):
-            nc.vector.tensor_tensor(
-                w[h][:], r[:, :, h * P : (h + 1) * P, :].rearrange("p u q e -> p q u e"), vs_by_slot, ALU.mult
-            )
+        for h in (1, 0):
+            nc.vector.tensor_tensor(w[h][:], r[h][:].rearrange("p u (q e) -> p q u e", e=2), vs_by_slot, ALU.mult)
 
         total = sb.tile([P, halves], F32, name="total")
         spent = sb.tile([P, halves, P], F32, name="spent")
-        for h in range(halves):
+        v_grouped = sb.tile([P, DV, PACK], BF16, name="v_grouped", tag="positive_then_grouped", align_bytes=64)
+        nc.scalar.copy(v_grouped[:], v_cols[:].rearrange("p t e -> p e t"))
+        for h in (1, 0):
             nc.scalar.activation(
                 spent[:, h, :], sums[h][:], ACT.Copy, bias=1.0 / (CAP * CAP * P), accum_out=total[:, h : h + 1]
             )
-        v_grouped = sb.tile([P, DV, PACK], BF16, name="v_grouped", align_bytes=64)
-        nc.scalar.copy(v_grouped[:], v_cols[:].rearrange("p t e -> p e t"))
 
         w_codes = [sb.tile([P, P], U32, name=f"w_codes{h}", align_bytes=64) for h in range(halves)]
         w_scales = [sb.tile([P, P], U8, name=f"w_scales{h}", align_bytes=64) for h in range(halves)]
         v_codes = sb.tile([P, DV], U32, name="v_codes", align_bytes=64)
         v_scales = sb.tile([P, DV], U8, name="v_scales", align_bytes=64)
         inverse = sb.tile([P, halves], F32, name="inverse")
-        nc.vector.quantize_mx(w_codes[0][:].bitcast(FP8X4), w_scales[0][:], w[0][:].rearrange("p q u e -> p (q u e)"))
-        nc.vector.quantize_mx(v_codes[:].bitcast(FP8X4), v_scales[:], v_grouped[:].rearrange("p e t -> p (e t)"))
         nc.vector.quantize_mx(w_codes[1][:].bitcast(FP8X4), w_scales[1][:], w[1][:].rearrange("p q u e -> p (q u e)"))
+        nc.vector.quantize_mx(v_codes[:].bitcast(FP8X4), v_scales[:], v_grouped[:].rearrange("p e t -> p (e t)"))
         nc.vector.reciprocal(inverse[:], total[:])
+        nc.vector.quantize_mx(w_codes[0][:].bitcast(FP8X4), w_scales[0][:], w[0][:].rearrange("p q u e -> p (q u e)"))
 
         y = [ps.tile([P, DV], F32, name=f"y{h}") for h in range(halves)]
         result = [sb.tile([P, DV], F32, name=f"result{h}") for h in range(halves)]
-        for h in range(halves):
+        for h in (1, 0):
             nc.tensor.matmul_mx(
                 out=y[h][:],
                 lhsT=w_codes[h][:].bitcast(FP8X4),
@@ -166,7 +168,7 @@ def tile_attend_rel2_cap_srtq256n512t1024_kernel(tc, q_words, q_scales, k_words,
                 start=True,
                 stop=True,
             )
-        nc.scalar.activation(result[0][:], y[0][:], ACT.Copy, scale=inverse[:, 0:1])
-        nc.scalar.dma_start(out[0, 0:P, :], result[0][:])
-        nc.vector.tensor_scalar(result[1][:], y[1][:], inverse[:, 1:2], None, ALU.mult)
-        nc.sync.dma_start(out[0, P:NQ, :], result[1][:])
+        nc.scalar.activation(result[1][:], y[1][:], ACT.Copy, scale=inverse[:, 1:2])
+        nc.scalar.dma_start(out[0, P:NQ, :], result[1][:])
+        nc.vector.tensor_scalar(result[0][:], y[0][:], inverse[:, 0:1], None, ALU.mult)
+        nc.sync.dma_start(out[0, 0:P, :], result[0][:])

@@ -34,11 +34,11 @@ def tile_attend_rel2_cap_srtq256n512t1024_kernel(tc, q_words, q_scales, k_words,
         ps = ctx.enter_context(tc.psum_pool(name="ps", bufs=1))
 
         offsets = sb.tile([P, N // 16], U16, name="offsets")
-        kw_pool = sb.tile([P, T], I32, name="kw_pool", tag="keys_then_scales", align_bytes=64)
+        kw_pool = sb.tile([P, T], I32, name="kw_pool", align_bytes=64)
         ks_pool = sb.tile([P, T], U8, name="ks_pool", align_bytes=64)
         qw = sb.tile([P, NQ], I32, name="qw", align_bytes=64)
         qs = sb.tile([P, NQ], U8, name="qs", align_bytes=64)
-        vs_pool = sb.tile([P, T], I32, name="vs_pool", tag="scales_then_values", align_bytes=64)
+        vs_pool = sb.tile([P, T], I32, name="vs_pool", align_bytes=64)
         warm = sb.tile([P, 8], F32, name="warm")
         warm2 = sb.tile([P, 8], F32, name="warm2")
 
@@ -71,16 +71,16 @@ def tile_attend_rel2_cap_srtq256n512t1024_kernel(tc, q_words, q_scales, k_words,
 
         ks_listed = sb.tile([P, N], U8, name="ks_listed", align_bytes=64)
         nc.vector.tensor_copy(ks_listed[:], ks_pool[:].indirect(offsets[:]))
-        kw = sb.tile([P, N], U32, name="kw", align_bytes=64)
-        nc.vector.tensor_copy(dealt(kw), kw_pool[:].bitcast(U32).indirect(offsets[:]))
         ks = sb.tile([P, N], U8, name="ks", align_bytes=64)
         nc.vector.tensor_copy(
             ks[:].bitcast(I32).rearrange("p (t b i) -> p t b i", t=PACK, i=2),
             ks_listed[:].bitcast(I32).rearrange("p (b t i) -> p t b i", t=PACK, i=2),
         )
-        vs_listed = sb.tile([P, N], U32, name="vs_listed", tag="keys_then_scales", align_bytes=64)
+        kw = sb.tile([P, N], U32, name="kw", align_bytes=64)
+        nc.vector.tensor_copy(dealt(kw), kw_pool[:].bitcast(U32).indirect(offsets[:]))
+        vs_listed = sb.tile([P, N], U32, name="vs_listed", align_bytes=64)
         nc.vector.tensor_copy(dealt(vs_listed), vs_pool[:].bitcast(U32).indirect(offsets[:]))
-        v_listed = sb.tile([P, N], BF16, name="v_listed", tag="scales_then_values", align_bytes=64)
+        v_listed = sb.tile([P, N], BF16, name="v_listed", align_bytes=64)
         nc.vector.tensor_copy(dealt(v_listed), v_pool[:].indirect(offsets[:]))
 
         score = [ps.tile([P, 2, NQ], F32, name=f"score{u}", tag=f"bank{u}") for u in range(2)]
@@ -111,8 +111,10 @@ def tile_attend_rel2_cap_srtq256n512t1024_kernel(tc, q_words, q_scales, k_words,
             nc.tensor.transpose(vs_cols[:, t, :], vs_listed[:, t * P : (t + 1) * P].bitcast(F32), ident32[:])
 
         positive = sb.tile([P, 2, 2 * P], F32, name="positive", tag="positive_then_grouped", align_bytes=64)
-        nc.scalar.activation(positive[:], th[0][:], ACT.Relu)
-        nc.scalar.activation(r[0][:], positive[:], ACT.Square)
+        for u in range(2):
+            nc.scalar.activation(positive[:, u], th[0][:, u], ACT.Relu)
+        for u in range(2):
+            nc.scalar.activation(r[0][:, u], positive[:, u], ACT.Square)
         nc.vector.scalar_tensor_tensor(r[1][:], th[1][:], 0.0, th[1][:], ALU.max, ALU.mult)
 
         v_cols = ps.tile([P, PACK, DV], BF16, name="v_cols", tag="bank1")

@@ -21,6 +21,9 @@ NQ = 256
 D = 512
 DV = 128
 CAP = 2.0
+HEAD_BLOCKS = 8
+V_HEAD = T - N + 32 * HEAD_BLOCKS
+XQ = 80
 
 FLOPS = 2 * NQ * N * (D + DV)
 
@@ -44,7 +47,8 @@ def tile_attend_rel2_cap_srtq256n512t1024_kernel(tc, q_words, q_scales, k_words,
 
         nc.gpsimd.memset(ks_pool[:].bitcast(I32), 0)
         nc.gpsimd.memset(qs[:].bitcast(I32), 0)
-        nc.vector.memset(vs_pool[:], 0)
+        nc.vector.memset(vs_pool[:, 0 : T // 2], 0)
+        nc.gpsimd.memset(vs_pool[:, T // 2 : T], 0)
         nc.gpsimd.memset(warm[:], 0.0)
 
         v_pool = sb.tile([P, T], F32, name="v_pool", align_bytes=64)
@@ -53,13 +57,20 @@ def tile_attend_rel2_cap_srtq256n512t1024_kernel(tc, q_words, q_scales, k_words,
             queue = nc.sync if j < 2 else nc.scalar
             queue.dma_start(ks_pool[j:P:32, :].bitcast(I32), k_scales[0, j:16:4, :].bitcast(I32))
         nc.sync.dma_start(kw_pool[:], k_words[0].rearrange("p n t -> p (n t)").bitcast(I32))
-        nc.sync.dma_start(qw[:], q_words[0, 0].rearrange("p n t -> p (n t)").bitcast(I32))
+        nc.sync.dma_start(v_pool[:, 0:V_HEAD], vT[:, 0:V_HEAD])
         nc.sync.dma_start(vs_pool[0:1, :], vs[0:1, :].bitcast(I32))
-        nc.sync.dma_start(v_pool[:], vT)
+        nc.sync.dma_start(qw[:], q_words[0, 0].rearrange("p n t -> p (n t)").bitcast(I32))
+
+        def load_qs(queue, j):
+            queue.dma_start(qs[j:P:32, :].bitcast(I32), q_scales[0, 0, j:16:4, :].bitcast(I32))
+
+        load_qs(nc.scalar, 2)
+        load_qs(nc.gpsimd, 0)
+        load_qs(nc.gpsimd, 1)
+        nc.sync.dma_start(v_pool[:, V_HEAD:T], vT[:, V_HEAD:T])
 
         nc.scalar.activation(warm2[:], warm[:], ACT.Tanh)
-        for j in range(4):
-            nc.scalar.dma_start(qs[j:P:32, :].bitcast(I32), q_scales[0, 0, j:16:4, :].bitcast(I32))
+        load_qs(nc.scalar, 3)
 
         ident32 = sb.tile([P, P], F32, name="ident32")
         make_identity(nc, ident32[:])
@@ -81,43 +92,57 @@ def tile_attend_rel2_cap_srtq256n512t1024_kernel(tc, q_words, q_scales, k_words,
         vs_listed = sb.tile([P, N], U32, name="vs_listed", align_bytes=64)
         nc.vector.tensor_copy(dealt(vs_listed), vs_pool[:].bitcast(U32).indirect(offsets[:]))
         v_listed = sb.tile([P, N], BF16, name="v_listed", align_bytes=64)
-        nc.vector.tensor_copy(dealt(v_listed), v_pool[:].indirect(offsets[:]))
+        v_head = sb.tile([P, V_HEAD], BF16, name="v_head", align_bytes=64)
+        nc.scalar.activation(v_head[:], v_pool[:, 0:V_HEAD], ACT.Copy)
+        nc.scalar.activation(
+            dealt(v_listed)[:, 0:HEAD_BLOCKS], v_head[:].indirect(offsets[:, 0 : 2 * HEAD_BLOCKS]), ACT.Copy
+        )
+        nc.vector.tensor_copy(dealt(v_listed)[:, HEAD_BLOCKS:], v_pool[:].indirect(offsets[:, 2 * HEAD_BLOCKS :]))
 
-        score = [ps.tile([P, 2, NQ], F32, name=f"score{u}", tag=f"bank{u}") for u in range(2)]
-        for t in range(PACK):
-            cols = slice(t * P, (t + 1) * P)
-            nc.tensor.matmul_mx(
-                out=score[t // 2][:, t % 2, :],
-                lhsT=kw[:, cols].bitcast(FP8X4),
-                lhsT_scale=ks[:, cols],
-                rhs=qw[:].bitcast(FP8X4),
-                rhs_scale=qs[:],
-                start=True,
-                stop=True,
-            )
+        score0 = ps.tile([P, PACK, P], F32, name="score0", tag="bank0")
+        score1 = [ps.tile([P, 2, P], F32, name=f"score1{u}", tag=f"bank1{u}") for u in range(2)]
+        for h in (1, 0):
+            for t in range(PACK):
+                cols = slice(t * P, (t + 1) * P)
+                nc.tensor.matmul_mx(
+                    out=score1[t // 2][:, t % 2, :] if h else score0[:, t, :],
+                    lhsT=kw[:, cols].bitcast(FP8X4),
+                    lhsT_scale=ks[:, cols],
+                    rhs=qw[:, h * P : (h + 1) * P].bitcast(FP8X4),
+                    rhs_scale=qs[:, h * P : (h + 1) * P],
+                    start=True,
+                    stop=True,
+                )
 
-        th_all = sb.tile([P, halves, 2, 2 * P], F32, name="th_all")
-        th = [th_all[:, h] for h in range(halves)]
+        th = [sb.tile([P, 2, 2 * P], F32, name=f"th{h}") for h in range(halves)]
         r = [sb.tile([P, 2, 2 * P], F32, name=f"r{h}") for h in range(halves)]
         for u in range(2):
             nc.scalar.activation(
-                th_all[:, :, u, :].rearrange("p h (q e) -> p h q e", e=2),
-                score[u][:].rearrange("p e (h q) -> p h q e", h=halves),
+                th[1][:, u].rearrange("p (q e) -> p q e", e=2),
+                score1[u][:].rearrange("p e q -> p q e"),
                 ACT.Tanh,
                 scale=1.0 / CAP,
             )
-        vs_cols = ps.tile([P, PACK, P], F32, name="vs_cols", tag="bank0")
+        nc.scalar.activation(
+            th[0][:].rearrange("p u (q e) -> p u q e", e=2),
+            score0[:].rearrange("p (u e) q -> p u q e", e=2),
+            ACT.Tanh,
+            scale=1.0 / CAP,
+        )
+        vs_cols = ps.tile([P, PACK, P], F32, name="vs_cols", tag="bank10")
         for t in range(PACK):
             nc.tensor.transpose(vs_cols[:, t, :], vs_listed[:, t * P : (t + 1) * P].bitcast(F32), ident32[:])
 
         positive = sb.tile([P, 2, 2 * P], F32, name="positive", tag="positive_then_grouped", align_bytes=64)
         for u in range(2):
-            nc.scalar.activation(positive[:, u], th[0][:, u], ACT.Relu)
+            nc.scalar.activation(positive[:, u, 2 * XQ :], th[0][:, u, 2 * XQ :], ACT.Relu)
         for u in range(2):
-            nc.scalar.activation(r[0][:, u], positive[:, u], ACT.Square)
-        nc.vector.scalar_tensor_tensor(r[1][:], th[1][:], 0.0, th[1][:], ALU.max, ALU.mult)
+            nc.scalar.activation(r[0][:, u, 2 * XQ :], positive[:, u, 2 * XQ :], ACT.Square)
+        for u in range(2):
+            nc.vector.scalar_tensor_tensor(r[1][:, u], th[1][:, u], 0.0, th[1][:, u], ALU.max, ALU.mult)
+        nc.vector.scalar_tensor_tensor(r[0][:, :, : 2 * XQ], th[0][:, :, : 2 * XQ], 0.0, th[0][:, :, : 2 * XQ], ALU.max, ALU.mult)
 
-        v_cols = ps.tile([P, PACK, DV], BF16, name="v_cols", tag="bank1")
+        v_cols = ps.tile([P, PACK, DV], BF16, name="v_cols", tag="bank0")
         for t in range(PACK):
             nc.tensor.transpose(v_cols[:, t, :], v_listed[:, t * P : (t + 1) * P], ident16[:])
 

@@ -42,14 +42,11 @@ def tile_attend_rel2_cap_srtq256n512t1024_kernel(tc, q_words, q_scales, k_words,
         qw = sb.tile([P, NQ], I32, name="qw", align_bytes=64)
         qs = sb.tile([P, NQ], U8, name="qs", align_bytes=64)
         vs_pool = sb.tile([P, T], I32, name="vs_pool", align_bytes=64)
-        warm = sb.tile([P, 8], F32, name="warm")
-        warm2 = sb.tile([P, 8], F32, name="warm2")
 
         nc.gpsimd.memset(ks_pool[:].bitcast(I32), 0)
         nc.gpsimd.memset(qs[:].bitcast(I32), 0)
         nc.vector.memset(vs_pool[:, 0 : T // 2], 0)
         nc.gpsimd.memset(vs_pool[:, T // 2 : T], 0)
-        nc.gpsimd.memset(warm[:], 0.0)
 
         v_pool = sb.tile([P, T], F32, name="v_pool", align_bytes=64)
         nc.sync.dma_start(offsets[:], offs)
@@ -69,7 +66,6 @@ def tile_attend_rel2_cap_srtq256n512t1024_kernel(tc, q_words, q_scales, k_words,
         load_qs(nc.gpsimd, 1)
         nc.sync.dma_start(v_pool[:, V_HEAD:T], vT[:, V_HEAD:T])
 
-        nc.scalar.activation(warm2[:], warm[:], ACT.Tanh)
         load_qs(nc.scalar, 3)
 
         ident32 = sb.tile([P, P], F32, name="ident32")

from contextlib import ExitStack

import concourse.mybir as mybir
from concourse.masks import make_identity

F32 = mybir.dt.float32
BF16 = mybir.dt.bfloat16
I32 = mybir.dt.int32
U32 = mybir.dt.uint32
U16 = mybir.dt.uint16
U8 = mybir.dt.uint8
FP8X4 = mybir.dt.float8_e4m3fn_x4
ACT = mybir.ActivationFunctionType
ALU = mybir.AluOpType

P = 128
PACK = 4
T = 1024
N = 512
NQ = 256
D = 512
DV = 128
CAP = 2.0
HEAD_BLOCKS = 8
V_HEAD = T - N + 32 * HEAD_BLOCKS
XQ = 80

FLOPS = 2 * NQ * N * (D + DV)


def tile_attend_rel2_cap_srtq256n512t1024_kernel(tc, q_words, q_scales, k_words, k_scales, vT, vs, offs, out):
    nc = tc.nc
    halves = NQ // P

    with ExitStack() as ctx:
        sb = ctx.enter_context(tc.tile_pool(name="sb", bufs=1))
        ps = ctx.enter_context(tc.psum_pool(name="ps", bufs=1))

        offsets = sb.tile([P, N // 16], U16, name="offsets")
        kw_pool = sb.tile([P, T], I32, name="kw_pool", align_bytes=64)
        ks_pool = sb.tile([P, T], U8, name="ks_pool", align_bytes=64)
        qw = sb.tile([P, NQ], I32, name="qw", align_bytes=64)
        qs = sb.tile([P, NQ], U8, name="qs", align_bytes=64)
        vs_pool = sb.tile([P, T], I32, name="vs_pool", align_bytes=64)

        nc.gpsimd.memset(ks_pool[:].bitcast(I32), 0)
        nc.gpsimd.memset(qs[:].bitcast(I32), 0)
        nc.vector.memset(vs_pool[:, 0 : T // 2], 0)
        nc.gpsimd.memset(vs_pool[:, T // 2 : T], 0)

        v_pool = sb.tile([P, T], F32, name="v_pool", align_bytes=64)
        nc.sync.dma_start(offsets[:], offs)
        for j in range(4):
            queue = nc.sync if j < 2 else nc.scalar
            queue.dma_start(ks_pool[j:P:32, :].bitcast(I32), k_scales[0, j:16:4, :].bitcast(I32))
        nc.sync.dma_start(kw_pool[:], k_words[0].rearrange("p n t -> p (n t)").bitcast(I32))
        nc.sync.dma_start(v_pool[:, 0:V_HEAD], vT[:, 0:V_HEAD])
        nc.sync.dma_start(vs_pool[0:1, :], vs[0:1, :].bitcast(I32))
        nc.sync.dma_start(qw[:], q_words[0, 0].rearrange("p n t -> p (n t)").bitcast(I32))

        def load_qs(queue, j):
            queue.dma_start(qs[j:P:32, :].bitcast(I32), q_scales[0, 0, j:16:4, :].bitcast(I32))

        load_qs(nc.scalar, 2)
        load_qs(nc.gpsimd, 0)
        load_qs(nc.gpsimd, 1)
        nc.sync.dma_start(v_pool[:, V_HEAD:T], vT[:, V_HEAD:T])

        load_qs(nc.scalar, 3)

        ident32 = sb.tile([P, P], F32, name="ident32")
        make_identity(nc, ident32[:])
        ident16 = sb.tile([P, P], BF16, name="ident16")
        make_identity(nc, ident16[:])

        def dealt(tile):
            return tile[:].rearrange("p (t b i) -> p b t i", t=PACK, i=8)

        ks_listed = sb.tile([P, N], U8, name="ks_listed", align_bytes=64)
        nc.vector.tensor_copy(ks_listed[:], ks_pool[:].indirect(offsets[:]))
        ks = sb.tile([P, N], U8, name="ks", align_bytes=64)
        nc.vector.tensor_copy(
            ks[:].bitcast(I32).rearrange("p (t b i) -> p t b i", t=PACK, i=2),
            ks_listed[:].bitcast(I32).rearrange("p (b t i) -> p t b i", t=PACK, i=2),
        )
        kw = sb.tile([P, N], U32, name="kw", align_bytes=64)
        nc.vector.tensor_copy(dealt(kw), kw_pool[:].bitcast(U32).indirect(offsets[:]))
        vs_listed = sb.tile([P, N], U32, name="vs_listed", align_bytes=64)
        nc.vector.tensor_copy(dealt(vs_listed), vs_pool[:].bitcast(U32).indirect(offsets[:]))
        v_listed = sb.tile([P, N], BF16, name="v_listed", align_bytes=64)
        v_head = sb.tile([P, V_HEAD], BF16, name="v_head", align_bytes=64)
        nc.scalar.activation(v_head[:], v_pool[:, 0:V_HEAD], ACT.Copy)
        nc.scalar.activation(
            dealt(v_listed)[:, 0:HEAD_BLOCKS], v_head[:].indirect(offsets[:, 0 : 2 * HEAD_BLOCKS]), ACT.Copy
        )
        nc.vector.tensor_copy(dealt(v_listed)[:, HEAD_BLOCKS:], v_pool[:].indirect(offsets[:, 2 * HEAD_BLOCKS :]))

        score0 = ps.tile([P, PACK, P], F32, name="score0", tag="bank0")
        score1 = [ps.tile([P, 2, P], F32, name=f"score1{u}", tag=f"bank1{u}") for u in range(2)]
        for h in (1, 0):
            for t in range(PACK):
                cols = slice(t * P, (t + 1) * P)
                nc.tensor.matmul_mx(
                    out=score1[t // 2][:, t % 2, :] if h else score0[:, t, :],
                    lhsT=kw[:, cols].bitcast(FP8X4),
                    lhsT_scale=ks[:, cols],
                    rhs=qw[:, h * P : (h + 1) * P].bitcast(FP8X4),
                    rhs_scale=qs[:, h * P : (h + 1) * P],
                    start=True,
                    stop=True,
                )

        th = [sb.tile([P, 2, 2 * P], F32, name=f"th{h}") for h in range(halves)]
        r = [sb.tile([P, 2, 2 * P], F32, name=f"r{h}") for h in range(halves)]
        for u in range(2):
            nc.scalar.activation(
                th[1][:, u].rearrange("p (q e) -> p q e", e=2),
                score1[u][:].rearrange("p e q -> p q e"),
                ACT.Tanh,
                scale=1.0 / CAP,
            )
        nc.scalar.activation(
            th[0][:].rearrange("p u (q e) -> p u q e", e=2),
            score0[:].rearrange("p (u e) q -> p u q e", e=2),
            ACT.Tanh,
            scale=1.0 / CAP,
        )
        vs_cols = ps.tile([P, PACK, P], F32, name="vs_cols", tag="bank10")
        for t in range(PACK):
            nc.tensor.transpose(vs_cols[:, t, :], vs_listed[:, t * P : (t + 1) * P].bitcast(F32), ident32[:])

        positive = sb.tile([P, 2, 2 * P], F32, name="positive", tag="positive_then_grouped", align_bytes=64)
        for u in range(2):
            nc.scalar.activation(positive[:, u, 2 * XQ :], th[0][:, u, 2 * XQ :], ACT.Relu)
        for u in range(2):
            nc.scalar.activation(r[0][:, u, 2 * XQ :], positive[:, u, 2 * XQ :], ACT.Square)
        for u in range(2):
            nc.vector.scalar_tensor_tensor(r[1][:, u], th[1][:, u], 0.0, th[1][:, u], ALU.max, ALU.mult)
        nc.vector.scalar_tensor_tensor(r[0][:, :, : 2 * XQ], th[0][:, :, : 2 * XQ], 0.0, th[0][:, :, : 2 * XQ], ALU.max, ALU.mult)

        v_cols = ps.tile([P, PACK, DV], BF16, name="v_cols", tag="bank0")
        for t in range(PACK):
            nc.tensor.transpose(v_cols[:, t, :], v_listed[:, t * P : (t + 1) * P], ident16[:])

        sums = [ps.tile([P, P], F32, name=f"sums{h}") for h in range(halves)]
        for h in (1, 0):
            for u in range(2):
                for e in range(2):
                    nc.tensor.matmul(
                        sums[h][:],
                        r[h][:, u, e : 2 * P : 2],
                        ident32[:],
                        start=(u == 0 and e == 0),
                        stop=(u == 1 and e == 1),
                        is_transpose=True,
                    )

        w = [sb.tile([P, P, 2, 2], BF16, name=f"w{h}", align_bytes=64) for h in range(halves)]
        vs_by_slot = vs_cols[:, :, 0:1].rearrange("p (u e) x -> p x u e", u=2).to_broadcast([P, P, 2, 2])
        for h in (1, 0):
            nc.vector.tensor_tensor(w[h][:], r[h][:].rearrange("p u (q e) -> p q u e", e=2), vs_by_slot, ALU.mult)

        total = sb.tile([P, halves], F32, name="total")
        spent = sb.tile([P, halves, P], F32, name="spent")
        v_grouped = sb.tile([P, DV, PACK], BF16, name="v_grouped", tag="positive_then_grouped", align_bytes=64)
        nc.scalar.copy(v_grouped[:], v_cols[:].rearrange("p t e -> p e t"))
        for h in (1, 0):
            nc.scalar.activation(
                spent[:, h, :], sums[h][:], ACT.Copy, bias=1.0 / (CAP * CAP * P), accum_out=total[:, h : h + 1]
            )

        w_codes = [sb.tile([P, P], U32, name=f"w_codes{h}", align_bytes=64) for h in range(halves)]
        w_scales = [sb.tile([P, P], U8, name=f"w_scales{h}", align_bytes=64) for h in range(halves)]
        v_codes = sb.tile([P, DV], U32, name="v_codes", align_bytes=64)
        v_scales = sb.tile([P, DV], U8, name="v_scales", align_bytes=64)
        inverse = sb.tile([P, halves], F32, name="inverse")
        nc.vector.quantize_mx(w_codes[1][:].bitcast(FP8X4), w_scales[1][:], w[1][:].rearrange("p q u e -> p (q u e)"))
        nc.vector.quantize_mx(v_codes[:].bitcast(FP8X4), v_scales[:], v_grouped[:].rearrange("p e t -> p (e t)"))
        nc.vector.reciprocal(inverse[:], total[:])
        nc.vector.quantize_mx(w_codes[0][:].bitcast(FP8X4), w_scales[0][:], w[0][:].rearrange("p q u e -> p (q u e)"))

        y = [ps.tile([P, DV], F32, name=f"y{h}") for h in range(halves)]
        result = [sb.tile([P, DV], F32, name=f"result{h}") for h in range(halves)]
        for h in (1, 0):
            nc.tensor.matmul_mx(
                out=y[h][:],
                lhsT=w_codes[h][:].bitcast(FP8X4),
                lhsT_scale=w_scales[h][:],
                rhs=v_codes[:].bitcast(FP8X4),
                rhs_scale=v_scales[:],
                start=True,
                stop=True,
            )
        nc.scalar.activation(result[1][:], y[1][:], ACT.Copy, scale=inverse[:, 1:2])
        nc.scalar.dma_start(out[0, P:NQ, :], result[1][:])
        nc.vector.tensor_scalar(result[0][:], y[0][:], inverse[:, 0:1], None, ALU.mult)
        nc.sync.dma_start(out[0, 0:P, :], result[0][:])
